import numpy as np
import ml_dtypes


def mxq(x, axis, fmt="e4m3"):
    dtype, down = {"e4m3": (ml_dtypes.float8_e4m3fn, 7), "e5m2": (ml_dtypes.float8_e5m2, 14)}[fmt]
    v = np.moveaxis(np.asarray(x, np.float32).astype(ml_dtypes.bfloat16).astype(np.float64), axis, -1)
    blocks = v.reshape(v.shape[:-1] + (-1, 32))
    amax = np.abs(blocks).max(-1, keepdims=True)
    byte = np.maximum(np.where(amax > 0, np.frexp(amax)[1] - 1 + 127, 0) - down, 1)
    scale = np.exp2(byte - 127.0)
    codes = (blocks / scale).astype(np.float32).astype(dtype).astype(np.float64)
    return np.moveaxis((codes * scale).reshape(v.shape), -1, axis)


WIDE = False


def mx_kscale(k):
    if not WIDE:
        return np.ones(k)
    levels = np.array([30, -30])
    if k % 512:
        return np.exp2(np.random.permutation(np.resize(levels, k // 32))).repeat(32)
    a = np.empty((k // 512, 16))
    for p in range(k // 512):
        a[p, :8] = np.random.permutation(np.resize(levels, 8))
        for g in range(8):
            far = levels[np.abs(levels - a[p, g]) >= 10]
            a[p, g + 8] = far[np.random.randint(len(far))]
    return np.exp2(a.ravel()).repeat(32)


def f64(x):
    return np.asarray(x).astype(np.float64)


def striped(idx):
    return np.tile(np.asarray(idx).reshape(-1, 16).T, (8, 1)).astype(np.uint16)


def unstriped(offs):
    return offs[:16].T.reshape(-1).astype(np.int64)


E2M1 = np.array([0.0, 0.5, 1.0, 1.5, 2.0, 3.0, 4.0, 6.0, -0.0, -0.5, -1.0, -1.5, -2.0, -3.0, -4.0, -6.0])


def pack_weight(w, fmt):
    k, n = w.shape
    w = f64(np.asarray(w, np.float32).astype(ml_dtypes.bfloat16)).reshape(k // 32, 32, n)
    amax = np.abs(w).max(1)
    if fmt == "e4m3":
        byte = np.frexp(amax)[1] - 1 + 127 - 7
    else:
        mant, ex = np.frexp(amax / 6.0)
        byte = np.where(mant > 0.5, ex, ex - 1) + 127
    byte = np.clip(np.where(amax > 0, byte, 1), 1, 254)
    scaled = (w * np.exp2(127.0 - byte)[:, None, :]).reshape(k, n).astype(np.float32)
    by_word = np.ascontiguousarray(scaled.reshape(k // 512, 128, 4, n).transpose(0, 1, 3, 2))
    if fmt == "e4m3":
        words = by_word.astype(ml_dtypes.float8_e4m3fn).view(np.uint8)
    else:
        c = by_word.astype(ml_dtypes.float4_e2m1fn).view(np.uint8) & 0xF
        words = (c[..., 0::2] | (c[..., 1::2] << 4)).reshape(k // 512, 128, 2 * n)
    return np.ascontiguousarray(words), np.ascontiguousarray(byte.astype(np.uint8).reshape(k // 512, 16, n))


def unpack_weight(words, scales, fmt):
    g, _, n = scales.shape
    words = np.ascontiguousarray(words).reshape(g, 128, n, -1)
    if fmt == "e4m3":
        vals = words.view(ml_dtypes.float8_e4m3fn).astype(np.float64)
    else:
        nib = np.empty((g, 128, n, 4), np.uint8)
        nib[..., 0::2] = words & 0xF
        nib[..., 1::2] = words >> 4
        vals = E2M1[nib]
    vals = vals * np.repeat(np.exp2(scales.astype(np.float64) - 127.0), 8, axis=1)[..., None]
    return vals.transpose(0, 1, 3, 2).reshape(g * 512, n)


K, J, N, R, T, V = 512, 512, 256, 256, 1024, 1024


def setup_inputs():
    n = np.random.standard_normal
    idx = np.random.permutation(T)[:J]
    idx2 = np.random.permutation(T)[:J]
    idx3 = np.random.permutation(V)[:J]
    fj = mx_kscale(J)
    fk = mx_kscale(K)
    drp = pack_weight(n((K, R)) * 1 / np.sqrt(K) / fk[:, None], "e4m3")
    return {
        "xf": (n((K, T))).astype(np.float32),
        "ra": (np.random.uniform(0.5, 1.5, (1, J)) * fj).astype(np.float32),
        "gt": (n((N, V)) * np.exp(0.5 * n((1, V)))).astype(np.float32),
        "rb": (np.random.uniform(0.5, 1.5, (1, J)) / fj).astype(np.float32),
        "cp": (np.random.uniform(0.4, 1.2, (N, 1))).astype(np.float32),
        "fkr": (np.random.uniform(0.5, 1.5, (1, K)) * fk).astype(np.float32),
        "dr_words": drp[0],
        "dr_scales": drp[1],
        "old": (1.0 * n((R, N))).astype(np.float32),
        "offs": striped(idx),
        "offs2": striped(idx2),
        "offs3": striped(idx3),
    }


def reference(xf, ra, gt, rb, cp, fkr, dr_words, dr_scales, old, offs, offs2, offs3):
    idx = unstriped(offs)
    idx2 = unstriped(offs2)
    idx3 = unstriped(offs3)
    dru = unpack_weight(dr_words, dr_scales, "e4m3")
    us = np.maximum(f64(xf)[:, idx], f64(xf)[:, idx2]) * f64(ra)
    ut = us.T
    uj = ut * f64(fkr)
    gs = np.minimum(f64(gt)[:, idx3], f64(cp)) * f64(rb)
    gj = gs.T
    ujq = mxq(uj, 0, "e4m3")
    gjq = mxq(gj, 0, "e5m2")
    w = ujq.T @ gjq
    wq = mxq(w, 0, "e5m2")
    v2 = dru.T @ wq
    y = 0.05 * v2 + 0.5 * f64(old)
    return y

@@ -1,0 +1,198 @@
+from contextlib import ExitStack
+
+import concourse.mybir as mybir
+from concourse.masks import make_identity
+
+K, J, N, R, T = 512, 512, 256, 256, 1024
+FLOPS = 2 * J * K * N + 2 * K * R * N
+
+F32 = mybir.dt.float32
+BF16 = mybir.dt.bfloat16
+I32 = mybir.dt.int32
+U32 = mybir.dt.uint32
+U16 = mybir.dt.uint16
+U8 = mybir.dt.uint8
+E4M3 = mybir.dt.float8_e4m3fn_x4
+E5M2 = mybir.dt.float8_e5m2_x4
+ALU = mybir.AluOpType
+COPY = mybir.ActivationFunctionType.Copy
+
+P = 128
+PACK = 4
+HALVES = N // P
+
+
+def tile_list_directions_larger_bounded_mixed_kernel(
+    tc, xf, ra, gt, rb, cp, fkr, dr_words, dr_scales, old, offs, offs2, offs3, out
+):
+    nc = tc.nc
+    with ExitStack() as ctx:
+        sb = ctx.enter_context(tc.tile_pool(name="sb", bufs=1))
+        ps = ctx.enter_context(tc.psum_pool(name="ps", bufs=1))
+
+        list1 = sb.tile([P, J // 16], U16, name="list1")
+        list2 = sb.tile([P, J // 16], U16, name="list2")
+        list3 = sb.tile([P, J // 16], U16, name="list3")
+        x = [sb.tile([P, T], F32, name="x%d" % t) for t in range(PACK)]
+        g = [sb.tile([P, T], F32, name="g%d" % h) for h in range(HALVES)]
+        ra_col = sb.tile([P, PACK], F32, name="ra_col")
+        rb_col = sb.tile([P, PACK], F32, name="rb_col")
+        fk_col = sb.tile([P, PACK], F32, name="fk_col")
+        cp_col = sb.tile([P, HALVES], F32, name="cp_col")
+        dr_codes = sb.tile([P, R], U32, name="dr_codes", align_bytes=64)
+        dr_plane = sb.tile([P, R], U8, name="dr_plane", align_bytes=64)
+        old_sb = sb.tile([P, R // P, N], F32, name="old_sb")
+        ident = sb.tile([P, P], F32, name="ident")
+
+        make_identity(nc, ident[:])
+        nc.vector.memset(dr_plane[:].bitcast(I32), 0)
+
+        x_rows = xf.rearrange("(p t) c -> t p c", t=PACK)
+        nc.sync.dma_start(list1[:], offs)
+        nc.sync.dma_start(list2[:], offs2)
+        nc.sync.dma_start(x[0][:], x_rows[0])
+        nc.scalar.dma_start(ra_col[:], ra.rearrange("o (p t) -> (o p) t", t=PACK))
+        nc.scalar.dma_start(fk_col[:], fkr.rearrange("o (p t) -> (o p) t", t=PACK))
+        for t in range(1, PACK):
+            nc.sync.dma_start(x[t][:], x_rows[t])
+        nc.sync.dma_start(list3[:], offs3)
+        for h in range(HALVES):
+            nc.sync.dma_start(g[h][:], gt[h * P : (h + 1) * P, :])
+        nc.gpsimd.dma_start(rb_col[:], rb.rearrange("o (p t) -> (o p) t", t=PACK))
+        with nc.allow_non_contiguous_dma(reason="one bound a partition and half"):
+            nc.gpsimd.dma_start(cp_col[:], cp.rearrange("(h p) o -> p (h o)", p=P))
+        nc.sync.dma_start(old_sb[:], old.rearrange("(a p) n -> p a n", p=P))
+        nc.sync.dma_start(
+            dr_codes[:].bitcast(I32), dr_words[0].rearrange("p c b -> p (c b)").bitcast(I32)
+        )
+        for q in range(4):
+            nc.sync.dma_start(
+                dr_plane[32 * q : 32 * q + 4, :].bitcast(I32),
+                dr_scales[0, 4 * q : 4 * q + 4, :].bitcast(I32),
+            )
+
+        def spread(col, name):
+            bank = ps.tile([P, PACK, P], F32, name=name, tag=name)
+            for m in range(PACK):
+                nc.tensor.transpose(bank[:, m, :], col[:, m : m + 1].to_broadcast([P, P]), ident[:])
+            return bank[:].rearrange("p m n -> p n m")
+
+        def gather(engine, tables, offsets, name):
+            picked = sb.tile([P, len(tables), J], F32, name=name, tag=name, align_bytes=64)
+            for i, table in enumerate(tables):
+                if engine == "scalar":
+                    nc.scalar.activation(picked[:, i, :], table[:].indirect(offsets[:]), COPY)
+                else:
+                    nc.vector.tensor_copy(picked[:, i, :], table[:].indirect(offsets[:]))
+            return picked
+
+        def larger_of(a, b, name):
+            count = a.shape[1]
+            larger = sb.tile([P, count, J], F32, name=name, tag=name)
+            nc.vector.tensor_tensor(larger[:], a[:], b[:], ALU.max)
+            return [larger[:, i, :] for i in range(count)]
+
+        def weigh(values, col, op, row, turned, name, tag):
+            rounded = sb.tile([P, J], BF16, name=name, tag=tag)
+            nc.vector.scalar_tensor_tensor(
+                out=rounded[:].rearrange("p (n m) -> p n m", m=PACK),
+                in0=values.rearrange("p (n m) -> p n m", m=PACK),
+                scalar=col,
+                in1=row,
+                op0=op,
+                op1=ALU.mult,
+            )
+            words = rounded[:].bitcast(F32)
+            for u in range(2):
+                nc.tensor.transpose(turned[:, u, :], words[:, u::2], ident[:])
+
+        def empty(bank, count, name, tag):
+            grouped = sb.tile([P, count, P * PACK], BF16, name=name, tag=tag, align_bytes=64)
+            nc.scalar.copy(
+                grouped[:].bitcast(F32).rearrange("p i (r u) -> p i r u", u=2),
+                bank[:].rearrange("p i u r -> p i r u"),
+            )
+            return grouped
+
+        def quantise(grouped, codes, fmt, name):
+            width = codes.shape[1]
+            plane = sb.tile([P, width], U8, name=name + "_plane", align_bytes=64)
+            nc.vector.quantize_mx(out=codes.bitcast(fmt), scales=plane[:], in_=grouped)
+            return [
+                (codes[:, c : c + P].bitcast(fmt), plane[:, c : c + P]) for c in range(0, width, P)
+            ]
+
+        def weigh_u(t, turned):
+            weigh(larger[t], fk_col[:, t : t + 1], ALU.mult, ra_row, turned, "u%d" % t, "u%d" % t)
+
+        def weigh_g(h, turned):
+            weigh(c[h][:, 0, :], cp_col[:, h : h + 1], ALU.min, rb_row, turned, "gs%d" % h, "larger%d" % (2 + h))
+
+        ra_row = spread(ra_col, "ra_bank")
+        rb_row = spread(rb_col, "rb_bank")
+        bank_a = ps.tile([P, 2, 2, P], F32, name="bank_a")
+        bank_b = ps.tile([P, 2, 2, P], F32, name="bank_b")
+        bank_c = ps.tile([P, 1, 2, P], F32, name="bank_c")
+        bank_d = ps.tile([P, 1, 2, P], F32, name="bank_d")
+
+        a01 = gather("scalar", x[0:2], list1, "a01")
+        b01 = gather("vector", x[0:2], list2, "b01")
+        a2 = gather("scalar", x[2:3], list1, "a2")
+        b2 = gather("vector", x[2:3], list2, "b2")
+        a3 = gather("scalar", x[3:4], list1, "a3")
+        b3 = gather("scalar", x[3:4], list2, "b3")
+        c = [gather("scalar", g[h : h + 1], list3, "c%d" % h) for h in range(HALVES)]
+
+        larger = larger_of(a01, b01, "larger01")
+        larger = larger + larger_of(a2, b2, "larger2")
+        weigh_u(0, bank_a[:, 0])
+        weigh_u(1, bank_a[:, 1])
+        larger = larger + larger_of(a3, b3, "larger3")
+        weigh_u(2, bank_b[:, 0])
+        weigh_u(3, bank_b[:, 1])
+        weigh_g(0, bank_c[:, 0])
+        weigh_g(1, bank_d[:, 0])
+
+        group_a = empty(bank_a, 2, "group_a", "group_a")
+        group_b = empty(bank_b, 2, "group_b", "group_b")
+        group_c = empty(bank_c, 1, "group_c", "group_c")
+        group_d = empty(bank_d, 1, "group_d", "group_d")
+        first_codes = sb.tile([P, (PACK + HALVES) * P], U32, name="first_codes", tag="c1", align_bytes=64)
+        uq = quantise(group_a[:].rearrange("p i c -> p (i c)"), first_codes[:, 0 : 2 * P], E4M3, "uq01")
+        uq = uq + quantise(group_b[:].rearrange("p i c -> p (i c)"), first_codes[:, 2 * P : 4 * P], E4M3, "uq23")
+        gq = quantise(group_c[:, 0, :], first_codes[:, 4 * P : 5 * P], E5M2, "gq0")
+        gq = gq + quantise(group_d[:, 0, :], first_codes[:, 5 * P : 6 * P], E5M2, "gq1")
+
+        old_half = sb.tile([P, R // P, N], F32, name="old_half", tag="group_d", align_bytes=64)
+        nc.vector.tensor_scalar_mul(old_half[:], old_sb[:], 0.5)
+        w = []
+        for h in range(HALVES):
+            w_bank = ps.tile([P, PACK, P], F32, name="w_bank%d" % h)
+            for t in range(PACK):
+                nc.tensor.matmul_mx(
+                    out=w_bank[:, t, :], lhsT=uq[t][0], lhsT_scale=uq[t][1],
+                    rhs=gq[h][0], rhs_scale=gq[h][1], start=True, stop=True,
+                )
+            w.append(sb.tile([P, P * PACK], BF16, name="w%d" % h, align_bytes=64))
+            nc.scalar.copy(
+                w[h][:].rearrange("p (n t) -> p n t", t=PACK), w_bank[:].rearrange("p t n -> p n t")
+            )
+        w_codes = sb.tile([P, N], U32, name="w_codes", align_bytes=64)
+        wq = [quantise(w[h][:], w_codes[:, h * P : (h + 1) * P], E5M2, "wq%d" % h)[0] for h in range(HALVES)]
+        for h in range(HALVES):
+            v_bank = ps.tile([P, R // P, P], F32, name="v_bank", tag=["ra_bank", "rb_bank"][h])
+            for i in range(R // P):
+                cols = slice(i * P, (i + 1) * P)
+                nc.tensor.matmul_mx(
+                    out=v_bank[:, i, :], lhsT=dr_codes[:, cols].bitcast(E4M3),
+                    lhsT_scale=dr_plane[:, cols], rhs=wq[h][0], rhs_scale=wq[h][1],
+                    start=True, stop=True,
+                )
+            res = sb.tile([P, R // P, P], F32, name="res%d" % h)
+            nc.vector.scalar_tensor_tensor(
+                out=res[:], in0=v_bank[:], scalar=0.05, in1=old_half[:, :, h * P : (h + 1) * P],
+                op0=ALU.mult, op1=ALU.add,
+            )
+            nc.sync.dma_start(
+                out[:, h * P : (h + 1) * P].rearrange("(a p) n -> p a n", p=P), res[:]
+            )

@@ -71,6 +71,10 @@ def tile_list_directions_larger_bounded_mixed_kernel(
                 dr_scales[0, 4 * q : 4 * q + 4, :].bitcast(I32),
             )
 
+        warm = sb.tile([P, 2], F32, name="warm")
+        nc.vector.memset(warm[:, 0:1], 0.0)
+        nc.scalar.activation(warm[:, 1:2], warm[:, 0:1], COPY)
+
         def spread(col, name):
             bank = ps.tile([P, PACK, P], F32, name=name, tag=name)
             for m in range(PACK):

@@ -53,14 +53,14 @@ def tile_list_directions_larger_bounded_mixed_kernel(
         nc.sync.dma_start(x[0][:], x_rows[0])
         nc.scalar.dma_start(ra_col[:], ra.rearrange("o (p t) -> (o p) t", t=PACK))
         nc.scalar.dma_start(fk_col[:], fkr.rearrange("o (p t) -> (o p) t", t=PACK))
+        nc.scalar.dma_start(rb_col[:], rb.rearrange("o (p t) -> (o p) t", t=PACK))
+        with nc.allow_non_contiguous_dma(reason="one bound a partition and half"):
+            nc.scalar.dma_start(cp_col[:], cp.rearrange("(h p) o -> p (h o)", p=P))
         for t in range(1, PACK):
             nc.sync.dma_start(x[t][:], x_rows[t])
         nc.sync.dma_start(list3[:], offs3)
         for h in range(HALVES):
             nc.sync.dma_start(g[h][:], gt[h * P : (h + 1) * P, :])
-        nc.gpsimd.dma_start(rb_col[:], rb.rearrange("o (p t) -> (o p) t", t=PACK))
-        with nc.allow_non_contiguous_dma(reason="one bound a partition and half"):
-            nc.gpsimd.dma_start(cp_col[:], cp.rearrange("(h p) o -> p (h o)", p=P))
         nc.sync.dma_start(old_sb[:], old.rearrange("(a p) n -> p a n", p=P))
         nc.sync.dma_start(
             dr_codes[:].bitcast(I32), dr_words[0].rearrange("p c b -> p (c b)").bitcast(I32)
@@ -76,10 +76,10 @@ def tile_list_directions_larger_bounded_mixed_kernel(
         nc.scalar.activation(warm[:, 1:2], warm[:, 0:1], COPY)
 
         def spread(col, name):
-            bank = ps.tile([P, PACK, P], F32, name=name, tag=name)
+            bank = ps.tile([P, J], F32, name=name, tag=name)
             for m in range(PACK):
-                nc.tensor.transpose(bank[:, m, :], col[:, m : m + 1].to_broadcast([P, P]), ident[:])
-            return bank[:].rearrange("p m n -> p n m")
+                nc.tensor.transpose(bank[:, m::PACK], col[:, m : m + 1].to_broadcast([P, P]), ident[:])
+            return bank[:]
 
         def gather(engine, tables, offsets, name):
             picked = sb.tile([P, len(tables), J], F32, name=name, tag=name, align_bytes=64)
@@ -92,31 +92,28 @@ def tile_list_directions_larger_bounded_mixed_kernel(
 
         def larger_of(a, b, name):
             count = a.shape[1]
-            larger = sb.tile([P, count, J], F32, name=name, tag=name)
+            larger = sb.tile([P, count, J], F32, name=name, tag=name, align_bytes=64)
             nc.vector.tensor_tensor(larger[:], a[:], b[:], ALU.max)
             return [larger[:, i, :] for i in range(count)]
 
-        def weigh(values, col, op, row, turned, name, tag):
-            rounded = sb.tile([P, J], BF16, name=name, tag=tag)
+        def weigh(values, col, op, row, rounded, turned):
             nc.vector.scalar_tensor_tensor(
-                out=rounded[:].rearrange("p (n m) -> p n m", m=PACK),
-                in0=values.rearrange("p (n m) -> p n m", m=PACK),
+                out=rounded,
+                in0=values,
                 scalar=col,
                 in1=row,
                 op0=op,
                 op1=ALU.mult,
             )
-            words = rounded[:].bitcast(F32)
+            words = rounded.bitcast(F32)
             for u in range(2):
                 nc.tensor.transpose(turned[:, u, :], words[:, u::2], ident[:])
 
-        def empty(bank, count, name, tag):
-            grouped = sb.tile([P, count, P * PACK], BF16, name=name, tag=tag, align_bytes=64)
+        def empty(bank, grouped):
             nc.scalar.copy(
-                grouped[:].bitcast(F32).rearrange("p i (r u) -> p i r u", u=2),
+                grouped.bitcast(F32).rearrange("p (i r u) -> p i r u", r=P, u=2),
                 bank[:].rearrange("p i u r -> p i r u"),
             )
-            return grouped
 
         def quantise(grouped, codes, fmt, name):
             width = codes.shape[1]
@@ -127,10 +124,11 @@ def tile_list_directions_larger_bounded_mixed_kernel(
             ]
 
         def weigh_u(t, turned):
-            weigh(larger[t], fk_col[:, t : t + 1], ALU.mult, ra_row, turned, "u%d" % t, "u%d" % t)
+            rounded = sb.tile([P, J], BF16, name="u%d" % t)
+            weigh(larger[t], fk_col[:, t : t + 1], ALU.mult, ra_row, rounded[:], turned)
 
-        def weigh_g(h, turned):
-            weigh(c[h][:, 0, :], cp_col[:, h : h + 1], ALU.min, rb_row, turned, "gs%d" % h, "larger%d" % (2 + h))
+        def weigh_g(h, rounded, turned):
+            weigh(c[h][:, 0, :], cp_col[:, h : h + 1], ALU.min, rb_row, rounded, turned)
 
         ra_row = spread(ra_col, "ra_bank")
         rb_row = spread(rb_col, "rb_bank")
@@ -148,24 +146,30 @@ def tile_list_directions_larger_bounded_mixed_kernel(
         c = [gather("scalar", g[h : h + 1], list3, "c%d" % h) for h in range(HALVES)]
 
         larger = larger_of(a01, b01, "larger01")
-        larger = larger + larger_of(a2, b2, "larger2")
         weigh_u(0, bank_a[:, 0])
+        larger = larger + larger_of(a2, b2, "larger2")
         weigh_u(1, bank_a[:, 1])
         larger = larger + larger_of(a3, b3, "larger3")
         weigh_u(2, bank_b[:, 0])
         weigh_u(3, bank_b[:, 1])
-        weigh_g(0, bank_c[:, 0])
-        weigh_g(1, bank_d[:, 0])
+        gs0 = sb.tile([P, J], BF16, name="gs0", tag="larger2", align_bytes=64)
+        late = sb.tile([P, 3 * J], BF16, name="late", tag="larger3", align_bytes=64)
+        weigh_g(0, gs0[:], bank_c[:, 0])
+        weigh_g(1, late[:, 2 * J : 3 * J], bank_d[:, 0])
 
-        group_a = empty(bank_a, 2, "group_a", "group_a")
-        group_b = empty(bank_b, 2, "group_b", "group_b")
-        group_c = empty(bank_c, 1, "group_c", "group_c")
-        group_d = empty(bank_d, 1, "group_d", "group_d")
-        first_codes = sb.tile([P, (PACK + HALVES) * P], U32, name="first_codes", tag="c1", align_bytes=64)
-        uq = quantise(group_a[:].rearrange("p i c -> p (i c)"), first_codes[:, 0 : 2 * P], E4M3, "uq01")
-        uq = uq + quantise(group_b[:].rearrange("p i c -> p (i c)"), first_codes[:, 2 * P : 4 * P], E4M3, "uq23")
-        gq = quantise(group_c[:, 0, :], first_codes[:, 4 * P : 5 * P], E5M2, "gq0")
-        gq = gq + quantise(group_d[:, 0, :], first_codes[:, 5 * P : 6 * P], E5M2, "gq1")
+        group_a = late[:, 0 : 2 * J]
+        group_b = sb.tile([P, 2 * J], BF16, name="group_b", align_bytes=64)
+        group_c = sb.tile([P, J], BF16, name="group_c", align_bytes=64)
+        group_d = sb.tile([P, J], BF16, name="group_d", tag="group_d", align_bytes=64)
+        empty(bank_a, group_a)
+        empty(bank_b, group_b[:])
+        empty(bank_c, group_c[:])
+        empty(bank_d, group_d[:])
+        first_codes = sb.tile([P, (PACK + HALVES) * P], U32, name="first_codes", align_bytes=64)
+        uq = quantise(group_a, first_codes[:, 0 : 2 * P], E4M3, "uq01")
+        uq = uq + quantise(group_b[:], first_codes[:, 2 * P : 4 * P], E4M3, "uq23")
+        gq = quantise(group_c[:], first_codes[:, 4 * P : 5 * P], E5M2, "gq0")
+        gq = gq + quantise(group_d[:], first_codes[:, 5 * P : 6 * P], E5M2, "gq1")
 
         old_half = sb.tile([P, R // P, N], F32, name="old_half", tag="group_d", align_bytes=64)
         nc.vector.tensor_scalar_mul(old_half[:], old_sb[:], 0.5)

@@ -48,19 +48,19 @@ def tile_list_directions_larger_bounded_mixed_kernel(
         nc.vector.memset(dr_plane[:].bitcast(I32), 0)
 
         x_rows = xf.rearrange("(p t) c -> t p c", t=PACK)
+        nc.sync.dma_start(x[0][:], x_rows[0])
         nc.sync.dma_start(list1[:], offs)
         nc.sync.dma_start(list2[:], offs2)
-        nc.sync.dma_start(x[0][:], x_rows[0])
         nc.scalar.dma_start(ra_col[:], ra.rearrange("o (p t) -> (o p) t", t=PACK))
         nc.scalar.dma_start(fk_col[:], fkr.rearrange("o (p t) -> (o p) t", t=PACK))
         nc.scalar.dma_start(rb_col[:], rb.rearrange("o (p t) -> (o p) t", t=PACK))
-        with nc.allow_non_contiguous_dma(reason="one bound a partition and half"):
-            nc.scalar.dma_start(cp_col[:], cp.rearrange("(h p) o -> p (h o)", p=P))
         for t in range(1, PACK):
             nc.sync.dma_start(x[t][:], x_rows[t])
         nc.sync.dma_start(list3[:], offs3)
         for h in range(HALVES):
             nc.sync.dma_start(g[h][:], gt[h * P : (h + 1) * P, :])
+        with nc.allow_non_contiguous_dma(reason="one bound a partition and half"):
+            nc.sync.dma_start(cp_col[:], cp.rearrange("(h p) o -> p (h o)", p=P))
         nc.sync.dma_start(old_sb[:], old.rearrange("(a p) n -> p a n", p=P))
         nc.sync.dma_start(
             dr_codes[:].bitcast(I32), dr_words[0].rearrange("p c b -> p (c b)").bitcast(I32)
@@ -77,9 +77,10 @@ def tile_list_directions_larger_bounded_mixed_kernel(
 
         def spread(col, name):
             bank = ps.tile([P, J], F32, name=name, tag=name)
+            places = bank[:].rearrange("p (u b c m) -> p m b u c", u=2, c=4, m=PACK)
             for m in range(PACK):
-                nc.tensor.transpose(bank[:, m::PACK], col[:, m : m + 1].to_broadcast([P, P]), ident[:])
-            return bank[:]
+                nc.tensor.transpose(places[:, m], col[:, m : m + 1].to_broadcast([P, P]), ident[:])
+            return bank[:].rearrange("p (u f) -> p u f", u=2)
 
         def gather(engine, tables, offsets, name):
             picked = sb.tile([P, len(tables), J], F32, name=name, tag=name, align_bytes=64)
@@ -92,22 +93,23 @@ def tile_list_directions_larger_bounded_mixed_kernel(
 
         def larger_of(a, b, name):
             count = a.shape[1]
-            larger = sb.tile([P, count, J], F32, name=name, tag=name, align_bytes=64)
-            nc.vector.tensor_tensor(larger[:], a[:], b[:], ALU.max)
-            return [larger[:, i, :] for i in range(count)]
-
-        def weigh(values, col, op, row, rounded, turned):
-            nc.vector.scalar_tensor_tensor(
-                out=rounded,
-                in0=values,
-                scalar=col,
-                in1=row,
-                op0=op,
-                op1=ALU.mult,
+            larger = sb.tile([P, 2, count, J // 2], F32, name=name, tag=name, align_bytes=64)
+            nc.vector.tensor_tensor(
+                larger[:].rearrange("p u i (b c) -> p u (i b) c", c=16),
+                a[:].rearrange("p i (b u c) -> p u (i b) c", u=2, c=16),
+                b[:].rearrange("p i (b u c) -> p u (i b) c", u=2, c=16),
+                ALU.max,
             )
+            return [larger[:, :, i, :] for i in range(count)]
+
+        def weigh(rounded, values, col, op, row):
+            nc.vector.scalar_tensor_tensor(
+                out=rounded, in0=values, scalar=col, in1=row, op0=op, op1=ALU.mult
+            )
+
+        def turn(rounded, u, turned):
             words = rounded.bitcast(F32)
-            for u in range(2):
-                nc.tensor.transpose(turned[:, u, :], words[:, u::2], ident[:])
+            nc.tensor.transpose(turned[:, u, :], words[:, u * P : (u + 1) * P], ident[:])
 
         def empty(bank, grouped):
             nc.scalar.copy(
@@ -125,15 +127,23 @@ def tile_list_directions_larger_bounded_mixed_kernel(
 
         def weigh_u(t, turned):
             rounded = sb.tile([P, J], BF16, name="u%d" % t)
-            weigh(larger[t], fk_col[:, t : t + 1], ALU.mult, ra_row, rounded[:], turned)
+            halves = rounded[:].rearrange("p (u f) -> p u f", u=2)
+            weigh(halves, larger[t], fk_col[:, t : t + 1], ALU.mult, ra_row)
+            for u in range(2):
+                turn(rounded[:], u, turned)
 
         def weigh_g(h, rounded, turned):
-            weigh(c[h][:, 0, :], cp_col[:, h : h + 1], ALU.min, rb_row, rounded, turned)
+            picked = c[h][:, 0, :].rearrange("p (b u c) -> p u b c", u=2, c=16)
+            halves = rounded.rearrange("p (u b c) -> p u b c", u=2, c=16)
+            row = rb_row.rearrange("p u (b c) -> p u b c", c=16)
+            for u in range(2):
+                weigh(halves[:, u], picked[:, u], cp_col[:, h : h + 1], ALU.min, row[:, u])
+                turn(rounded, u, turned)
 
         ra_row = spread(ra_col, "ra_bank")
         rb_row = spread(rb_col, "rb_bank")
-        bank_a = ps.tile([P, 2, 2, P], F32, name="bank_a")
-        bank_b = ps.tile([P, 2, 2, P], F32, name="bank_b")
+        bank_a = ps.tile([P, 2, 2, P], F32, name="bank_a", tag="bank_a")
+        bank_b = ps.tile([P, 2, 2, P], F32, name="bank_b", tag="bank_b")
         bank_c = ps.tile([P, 1, 2, P], F32, name="bank_c")
         bank_d = ps.tile([P, 1, 2, P], F32, name="bank_d")
 
@@ -165,7 +175,7 @@ def tile_list_directions_larger_bounded_mixed_kernel(
         empty(bank_b, group_b[:])
         empty(bank_c, group_c[:])
         empty(bank_d, group_d[:])
-        first_codes = sb.tile([P, (PACK + HALVES) * P], U32, name="first_codes", align_bytes=64)
+        first_codes = sb.tile([P, (PACK + HALVES) * P], U32, name="first_codes", tag="c1", align_bytes=64)
         uq = quantise(group_a, first_codes[:, 0 : 2 * P], E4M3, "uq01")
         uq = uq + quantise(group_b[:], first_codes[:, 2 * P : 4 * P], E4M3, "uq23")
         gq = quantise(group_c[:], first_codes[:, 4 * P : 5 * P], E5M2, "gq0")
@@ -187,20 +197,20 @@ def tile_list_directions_larger_bounded_mixed_kernel(
             )
         w_codes = sb.tile([P, N], U32, name="w_codes", align_bytes=64)
         wq = [quantise(w[h][:], w_codes[:, h * P : (h + 1) * P], E5M2, "wq%d" % h)[0] for h in range(HALVES)]
+        free_banks = [["ra_bank", "bank_a"], ["rb_bank", "bank_b"]]
         for h in range(HALVES):
-            v_bank = ps.tile([P, R // P, P], F32, name="v_bank", tag=["ra_bank", "rb_bank"][h])
+            n_cols = slice(h * P, (h + 1) * P)
             for i in range(R // P):
-                cols = slice(i * P, (i + 1) * P)
+                r_cols = slice(i * P, (i + 1) * P)
+                v_bank = ps.tile([P, P], F32, name="v_bank", tag=free_banks[h][i])
                 nc.tensor.matmul_mx(
-                    out=v_bank[:, i, :], lhsT=dr_codes[:, cols].bitcast(E4M3),
-                    lhsT_scale=dr_plane[:, cols], rhs=wq[h][0], rhs_scale=wq[h][1],
+                    out=v_bank[:], lhsT=dr_codes[:, r_cols].bitcast(E4M3),
+                    lhsT_scale=dr_plane[:, r_cols], rhs=wq[h][0], rhs_scale=wq[h][1],
                     start=True, stop=True,
                 )
-            res = sb.tile([P, R // P, P], F32, name="res%d" % h)
-            nc.vector.scalar_tensor_tensor(
-                out=res[:], in0=v_bank[:], scalar=0.05, in1=old_half[:, :, h * P : (h + 1) * P],
-                op0=ALU.mult, op1=ALU.add,
-            )
-            nc.sync.dma_start(
-                out[:, h * P : (h + 1) * P].rearrange("(a p) n -> p a n", p=P), res[:]
-            )
+                res = sb.tile([P, P], F32, name="res%d%d" % (h, i))
+                nc.vector.scalar_tensor_tensor(
+                    out=res[:], in0=v_bank[:], scalar=0.05, in1=old_half[:, i, n_cols],
+                    op0=ALU.mult, op1=ALU.add,
+                )
+                nc.sync.dma_start(out[r_cols, n_cols], res[:])

from contextlib import ExitStack

import concourse.mybir as mybir
from concourse.masks import make_identity

K, J, N, R, T = 512, 512, 256, 256, 1024
FLOPS = 2 * J * K * N + 2 * K * R * N

F32 = mybir.dt.float32
BF16 = mybir.dt.bfloat16
I32 = mybir.dt.int32
U32 = mybir.dt.uint32
U16 = mybir.dt.uint16
U8 = mybir.dt.uint8
E4M3 = mybir.dt.float8_e4m3fn_x4
E5M2 = mybir.dt.float8_e5m2_x4
ALU = mybir.AluOpType
COPY = mybir.ActivationFunctionType.Copy

P = 128
PACK = 4
HALVES = N // P


def tile_list_directions_larger_bounded_mixed_kernel(
    tc, xf, ra, gt, rb, cp, fkr, dr_words, dr_scales, old, offs, offs2, offs3, out
):
    nc = tc.nc
    with ExitStack() as ctx:
        sb = ctx.enter_context(tc.tile_pool(name="sb", bufs=1))
        ps = ctx.enter_context(tc.psum_pool(name="ps", bufs=1))

        list1 = sb.tile([P, J // 16], U16, name="list1")
        list2 = sb.tile([P, J // 16], U16, name="list2")
        list3 = sb.tile([P, J // 16], U16, name="list3")
        x = [sb.tile([P, T], F32, name="x%d" % t) for t in range(PACK)]
        g = [sb.tile([P, T], F32, name="g%d" % h) for h in range(HALVES)]
        ra_col = sb.tile([P, PACK], F32, name="ra_col")
        rb_col = sb.tile([P, PACK], F32, name="rb_col")
        fk_col = sb.tile([P, PACK], F32, name="fk_col")
        cp_col = sb.tile([P, HALVES], F32, name="cp_col")
        dr_codes = sb.tile([P, R], U32, name="dr_codes", align_bytes=64)
        dr_plane = sb.tile([P, R], U8, name="dr_plane", align_bytes=64)
        old_sb = sb.tile([P, R // P, N], F32, name="old_sb")
        ident = sb.tile([P, P], F32, name="ident")

        make_identity(nc, ident[:])
        nc.vector.memset(dr_plane[:].bitcast(I32), 0)

        x_rows = xf.rearrange("(p t) c -> t p c", t=PACK)
        nc.sync.dma_start(x[0][:], x_rows[0])
        nc.sync.dma_start(list1[:], offs)
        nc.sync.dma_start(list2[:], offs2)
        nc.scalar.dma_start(ra_col[:], ra.rearrange("o (p t) -> (o p) t", t=PACK))
        nc.scalar.dma_start(fk_col[:], fkr.rearrange("o (p t) -> (o p) t", t=PACK))
        nc.scalar.dma_start(rb_col[:], rb.rearrange("o (p t) -> (o p) t", t=PACK))
        for t in range(1, PACK):
            nc.sync.dma_start(x[t][:], x_rows[t])
        nc.sync.dma_start(list3[:], offs3)
        for h in range(HALVES):
            nc.sync.dma_start(g[h][:], gt[h * P : (h + 1) * P, :])
        with nc.allow_non_contiguous_dma(reason="one bound a partition and half"):
            nc.sync.dma_start(cp_col[:], cp.rearrange("(h p) o -> p (h o)", p=P))
        nc.sync.dma_start(old_sb[:], old.rearrange("(a p) n -> p a n", p=P))
        nc.sync.dma_start(
            dr_codes[:].bitcast(I32), dr_words[0].rearrange("p c b -> p (c b)").bitcast(I32)
        )
        for q in range(4):
            nc.sync.dma_start(
                dr_plane[32 * q : 32 * q + 4, :].bitcast(I32),
                dr_scales[0, 4 * q : 4 * q + 4, :].bitcast(I32),
            )

        warm = sb.tile([P, 2], F32, name="warm")
        nc.vector.memset(warm[:, 0:1], 0.0)
        nc.scalar.activation(warm[:, 1:2], warm[:, 0:1], COPY)

        def spread(col, name):
            bank = ps.tile([P, J], F32, name=name, tag=name)
            places = bank[:].rearrange("p (u b c m) -> p m b u c", u=2, c=4, m=PACK)
            for m in range(PACK):
                nc.tensor.transpose(places[:, m], col[:, m : m + 1].to_broadcast([P, P]), ident[:])
            return bank[:].rearrange("p (u f) -> p u f", u=2)

        def gather(engine, tables, offsets, name):
            picked = sb.tile([P, len(tables), J], F32, name=name, tag=name, align_bytes=64)
            for i, table in enumerate(tables):
                if engine == "scalar":
                    nc.scalar.activation(picked[:, i, :], table[:].indirect(offsets[:]), COPY)
                else:
                    nc.vector.tensor_copy(picked[:, i, :], table[:].indirect(offsets[:]))
            return picked

        def larger_of(a, b, name):
            count = a.shape[1]
            larger = sb.tile([P, 2, count, J // 2], F32, name=name, tag=name, align_bytes=64)
            nc.vector.tensor_tensor(
                larger[:].rearrange("p u i (b c) -> p u (i b) c", c=16),
                a[:].rearrange("p i (b u c) -> p u (i b) c", u=2, c=16),
                b[:].rearrange("p i (b u c) -> p u (i b) c", u=2, c=16),
                ALU.max,
            )
            return [larger[:, :, i, :] for i in range(count)]

        def weigh(rounded, values, col, op, row):
            nc.vector.scalar_tensor_tensor(
                out=rounded, in0=values, scalar=col, in1=row, op0=op, op1=ALU.mult
            )

        def turn(rounded, u, turned):
            words = rounded.bitcast(F32)
            nc.tensor.transpose(turned[:, u, :], words[:, u * P : (u + 1) * P], ident[:])

        def empty(bank, grouped):
            nc.scalar.copy(
                grouped.bitcast(F32).rearrange("p (i r u) -> p i r u", r=P, u=2),
                bank[:].rearrange("p i u r -> p i r u"),
            )

        def quantise(grouped, codes, fmt, name):
            width = codes.shape[1]
            plane = sb.tile([P, width], U8, name=name + "_plane", align_bytes=64)
            nc.vector.quantize_mx(out=codes.bitcast(fmt), scales=plane[:], in_=grouped)
            return [
                (codes[:, c : c + P].bitcast(fmt), plane[:, c : c + P]) for c in range(0, width, P)
            ]

        def weigh_u(t, turned):
            rounded = sb.tile([P, J], BF16, name="u%d" % t)
            halves = rounded[:].rearrange("p (u f) -> p u f", u=2)
            weigh(halves, larger[t], fk_col[:, t : t + 1], ALU.mult, ra_row)
            for u in range(2):
                turn(rounded[:], u, turned)

        def weigh_g(h, rounded, turned):
            picked = c[h][:, 0, :].rearrange("p (b u c) -> p u b c", u=2, c=16)
            halves = rounded.rearrange("p (u b c) -> p u b c", u=2, c=16)
            row = rb_row.rearrange("p u (b c) -> p u b c", c=16)
            for u in range(2):
                weigh(halves[:, u], picked[:, u], cp_col[:, h : h + 1], ALU.min, row[:, u])
                turn(rounded, u, turned)

        ra_row = spread(ra_col, "ra_bank")
        rb_row = spread(rb_col, "rb_bank")
        bank_a = ps.tile([P, 2, 2, P], F32, name="bank_a", tag="bank_a")
        bank_b = ps.tile([P, 2, 2, P], F32, name="bank_b", tag="bank_b")
        bank_c = ps.tile([P, 1, 2, P], F32, name="bank_c")
        bank_d = ps.tile([P, 1, 2, P], F32, name="bank_d")

        a01 = gather("scalar", x[0:2], list1, "a01")
        b01 = gather("vector", x[0:2], list2, "b01")
        a2 = gather("scalar", x[2:3], list1, "a2")
        b2 = gather("vector", x[2:3], list2, "b2")
        a3 = gather("scalar", x[3:4], list1, "a3")
        b3 = gather("scalar", x[3:4], list2, "b3")
        c = [gather("scalar", g[h : h + 1], list3, "c%d" % h) for h in range(HALVES)]

        larger = larger_of(a01, b01, "larger01")
        weigh_u(0, bank_a[:, 0])
        larger = larger + larger_of(a2, b2, "larger2")
        weigh_u(1, bank_a[:, 1])
        larger = larger + larger_of(a3, b3, "larger3")
        weigh_u(2, bank_b[:, 0])
        weigh_u(3, bank_b[:, 1])
        gs0 = sb.tile([P, J], BF16, name="gs0", tag="larger2", align_bytes=64)
        late = sb.tile([P, 3 * J], BF16, name="late", tag="larger3", align_bytes=64)
        weigh_g(0, gs0[:], bank_c[:, 0])
        weigh_g(1, late[:, 2 * J : 3 * J], bank_d[:, 0])

        group_a = late[:, 0 : 2 * J]
        group_b = sb.tile([P, 2 * J], BF16, name="group_b", align_bytes=64)
        group_c = sb.tile([P, J], BF16, name="group_c", align_bytes=64)
        group_d = sb.tile([P, J], BF16, name="group_d", tag="group_d", align_bytes=64)
        empty(bank_a, group_a)
        empty(bank_b, group_b[:])
        empty(bank_c, group_c[:])
        empty(bank_d, group_d[:])
        first_codes = sb.tile([P, (PACK + HALVES) * P], U32, name="first_codes", tag="c1", align_bytes=64)
        uq = quantise(group_a, first_codes[:, 0 : 2 * P], E4M3, "uq01")
        uq = uq + quantise(group_b[:], first_codes[:, 2 * P : 4 * P], E4M3, "uq23")
        gq = quantise(group_c[:], first_codes[:, 4 * P : 5 * P], E5M2, "gq0")
        gq = gq + quantise(group_d[:], first_codes[:, 5 * P : 6 * P], E5M2, "gq1")

        old_half = sb.tile([P, R // P, N], F32, name="old_half", tag="group_d", align_bytes=64)
        nc.vector.tensor_scalar_mul(old_half[:], old_sb[:], 0.5)
        w = []
        for h in range(HALVES):
            w_bank = ps.tile([P, PACK, P], F32, name="w_bank%d" % h)
            for t in range(PACK):
                nc.tensor.matmul_mx(
                    out=w_bank[:, t, :], lhsT=uq[t][0], lhsT_scale=uq[t][1],
                    rhs=gq[h][0], rhs_scale=gq[h][1], start=True, stop=True,
                )
            w.append(sb.tile([P, P * PACK], BF16, name="w%d" % h, align_bytes=64))
            nc.scalar.copy(
                w[h][:].rearrange("p (n t) -> p n t", t=PACK), w_bank[:].rearrange("p t n -> p n t")
            )
        w_codes = sb.tile([P, N], U32, name="w_codes", align_bytes=64)
        wq = [quantise(w[h][:], w_codes[:, h * P : (h + 1) * P], E5M2, "wq%d" % h)[0] for h in range(HALVES)]
        free_banks = [["ra_bank", "bank_a"], ["rb_bank", "bank_b"]]
        for h in range(HALVES):
            n_cols = slice(h * P, (h + 1) * P)
            for i in range(R // P):
                r_cols = slice(i * P, (i + 1) * P)
                v_bank = ps.tile([P, P], F32, name="v_bank", tag=free_banks[h][i])
                nc.tensor.matmul_mx(
                    out=v_bank[:], lhsT=dr_codes[:, r_cols].bitcast(E4M3),
                    lhsT_scale=dr_plane[:, r_cols], rhs=wq[h][0], rhs_scale=wq[h][1],
                    start=True, stop=True,
                )
                res = sb.tile([P, P], F32, name="res%d%d" % (h, i))
                nc.vector.scalar_tensor_tensor(
                    out=res[:], in0=v_bank[:], scalar=0.05, in1=old_half[:, i, n_cols],
                    op0=ALU.mult, op1=ALU.add,
                )
                nc.sync.dma_start(out[r_cols, n_cols], res[:])
